import numpy as np
import ml_dtypes


def mxq(x, axis, fmt="e4m3"):
    dtype, down = {"e4m3": (ml_dtypes.float8_e4m3fn, 7), "e5m2": (ml_dtypes.float8_e5m2, 14)}[fmt]
    v = np.moveaxis(np.asarray(x, np.float32).astype(ml_dtypes.bfloat16).astype(np.float64), axis, -1)
    blocks = v.reshape(v.shape[:-1] + (-1, 32))
    amax = np.abs(blocks).max(-1, keepdims=True)
    byte = np.maximum(np.where(amax > 0, np.frexp(amax)[1] - 1 + 127, 0) - down, 1)
    scale = np.exp2(byte - 127.0)
    codes = (blocks / scale).astype(np.float32).astype(dtype).astype(np.float64)
    return np.moveaxis((codes * scale).reshape(v.shape), -1, axis)


WIDE = False


def mx_kscale(k):
    if not WIDE:
        return np.ones(k)
    levels = np.array([10, -10, 5, -5, 0])
    if k % 512:
        return np.exp2(np.random.permutation(np.resize(levels, k // 32))).repeat(32)
    a = np.empty((k // 512, 16))
    for p in range(k // 512):
        a[p, :8] = np.random.permutation(np.resize(levels, 8))
        for g in range(8):
            far = levels[np.abs(levels - a[p, g]) >= 10]
            a[p, g + 8] = far[np.random.randint(len(far))]
    return np.exp2(a.ravel()).repeat(32)


def f64(x):
    return np.asarray(x).astype(np.float64)


def striped(idx):
    return np.tile(idx.reshape(-1, 16).T, (8, 1)).astype(np.uint16)


def unstriped(offs):
    return offs[:16].T.reshape(-1).astype(np.int64)


E2M1 = np.array([0.0, 0.5, 1.0, 1.5, 2.0, 3.0, 4.0, 6.0, -0.0, -0.5, -1.0, -1.5, -2.0, -3.0, -4.0, -6.0])


def pack_weight(w, fmt):
    k, n = w.shape
    w = f64(np.asarray(w, np.float32).astype(ml_dtypes.bfloat16)).reshape(k // 32, 32, n)
    amax = np.abs(w).max(1)
    if fmt == "e4m3":
        byte = np.frexp(amax)[1] - 1 + 127 - 7
    else:
        mant, ex = np.frexp(amax / 6.0)
        byte = np.where(mant > 0.5, ex, ex - 1) + 127
    byte = np.clip(np.where(amax > 0, byte, 1), 1, 254)
    scaled = (w * np.exp2(127.0 - byte)[:, None, :]).reshape(k, n).astype(np.float32)
    by_word = np.ascontiguousarray(scaled.reshape(k // 512, 128, 4, n).transpose(0, 1, 3, 2))
    if fmt == "e4m3":
        words = by_word.astype(ml_dtypes.float8_e4m3fn).view(np.uint8)
    else:
        c = by_word.astype(ml_dtypes.float4_e2m1fn).view(np.uint8) & 0xF
        words = (c[..., 0::2] | (c[..., 1::2] << 4)).reshape(k // 512, 128, 2 * n)
    return np.ascontiguousarray(words), np.ascontiguousarray(byte.astype(np.uint8).reshape(k // 512, 16, n))


def unpack_weight(words, scales, fmt):
    g, _, n = scales.shape
    words = np.ascontiguousarray(words).reshape(g, 128, n, -1)
    if fmt == "e4m3":
        vals = words.view(ml_dtypes.float8_e4m3fn).astype(np.float64)
    else:
        nib = np.empty((g, 128, n, 4), np.uint8)
        nib[..., 0::2] = words & 0xF
        nib[..., 1::2] = words >> 4
        vals = E2M1[nib]
    vals = vals * np.repeat(np.exp2(scales.astype(np.float64) - 127.0), 8, axis=1)[..., None]
    return vals.transpose(0, 1, 3, 2).reshape(g * 512, n)


K, T, E, C, N = 1024, 768, 12, 128, 128
R = 2


def by_expert(wq, xq):
    return np.concatenate([wq[e].T @ xq[:, e * C:(e + 1) * C] for e in range(E)], axis=1)


def setup_inputs():
    n = np.random.standard_normal
    s = mx_kscale(K)[:, None]
    slot_token = np.concatenate([r * (T // R) + np.random.permutation(T // R)[:C // R] for e in range(E) for r in range(R)])
    w = [pack_weight(m, "e2m1") for m in n((E, K, N)) / np.sqrt(K) / s[None]]
    return {
        "xT": (n((K, T)) * s).astype(np.float32),
        "w_words": np.stack([m[0] for m in w]),
        "w_scales": np.stack([m[1] for m in w]),
        "b": (0.3 * n((N, E))).astype(np.float32),
        "offs": striped(slot_token),
    }


def reference(xT, w_words, w_scales, b, offs):
    idx = unstriped(offs)
    w = np.stack([unpack_weight(w_words[e], w_scales[e], "e2m1") for e in range(E)])
    xq = mxq(f64(xT)[:, idx], 0, "e4m3")
    y = by_expert(w, xq)
    y = y + np.repeat(f64(b), C, axis=1)
    return y.reshape(N, E, R, C // R).transpose(0, 2, 1, 3).reshape(N, E * C)

@@ -1,0 +1,156 @@
+from contextlib import ExitStack
+
+import concourse.mybir as mybir
+
+K, T, E, C, N, R = 1024, 768, 12, 128, 128, 2
+P = 128
+PASSES = 2
+S = E * C
+U = C // R
+FLOPS = 2 * S * K * N
+
+F32 = mybir.dt.float32
+BF16 = mybir.dt.bfloat16
+I32 = mybir.dt.int32
+U32 = mybir.dt.uint32
+U16 = mybir.dt.uint16
+U8 = mybir.dt.uint8
+FP8X4 = mybir.dt.float8_e4m3fn_x4
+FP4X4 = mybir.dt.float4_e2m1fn_x4
+COPY = mybir.ActivationFunctionType.Copy
+IDENTITY = mybir.ActivationFunctionType.Identity
+
+W = 1024
+
+
+def tile_moe_eps_lin_bias_kernel(tc, xT, w_words, w_scales, b, offs, out):
+    nc = tc.nc
+    with ExitStack() as ctx:
+        keep = ctx.enter_context(tc.tile_pool(name="keep", bufs=1))
+        psum = ctx.enter_context(tc.psum_pool(name="psum", bufs=8))
+
+        offsets = keep.tile([P, S // 16], U16, name="offsets")
+        plane = keep.tile([P, W], U8, name="plane", align_bytes=64)
+        w_codes = keep.tile([P, E * PASSES, 2 * N], U8, name="w_codes", align_bytes=64)
+        w_plane = keep.tile([P, E * PASSES, N], U8, name="w_plane", align_bytes=64)
+        bias = keep.tile([P, E], F32, name="bias")
+        codes = [keep.tile([P, w], U32, name=f"codes{a}", align_bytes=64) for a, w in enumerate((2 * W, W))]
+        slot_codes = [keep.tile([P, S], U32, name=f"slot_codes{a}", align_bytes=64) for a in range(PASSES)]
+        slot_plane = keep.tile([P, S], U8, name="slot_plane", align_bytes=64)
+        slot_plane1 = keep.tile([P, S], U8, name="slot_plane1", align_bytes=64)
+        rounded = [keep.tile([P, T, 4], BF16, name=f"rounded{a}", align_bytes=64) for a in range(PASSES)]
+
+        nc.gpsimd.memset(plane[:].bitcast(I32), 0)
+        for a in range(PASSES):
+            nc.gpsimd.memset(codes[a][:, T:].bitcast(I32), 0)
+        nc.gpsimd.memset(slot_plane1[:].bitcast(I32), 0)
+        nc.gpsimd.memset(w_plane[:].rearrange("p a n -> p (a n)").bitcast(I32), 0)
+
+        raw = {}
+
+        def load(a, c0, c1):
+            t = keep.tile([P, 4, c1 - c0], F32, name=f"raw{a}_{c0}")
+            nc.sync.dma_start(t[:], xT[512 * a : 512 * a + 512, c0:c1].rearrange("(p j) w -> p j w", j=4))
+            raw[a, c0] = t
+
+        def cast(engine, a, base, c0, c1):
+            src = raw[a, base][:, :, c0 - base : c1 - base].rearrange("p j (c i) -> p c j i", i=4)
+            dst = rounded[a][:, c0:c1, :].rearrange("p (c i) j -> p c j i", i=4)
+            if engine == "v":
+                nc.vector.tensor_copy(dst, src)
+            else:
+                nc.scalar.activation(dst, src, COPY)
+
+        def quantise(a, c0, c1):
+            nc.vector.quantize_mx(
+                out=codes[a][:, c0:c1].bitcast(FP8X4),
+                scales=plane[4 * a : P, c0:c1],
+                in_=rounded[a][:, c0:c1, :].rearrange("p w j -> p (w j)"),
+            )
+
+        load(0, 0, 512)
+        load(0, 512, 768)
+        nc.sync.dma_start(offsets[:], offs)
+        load(1, 0, 256)
+        load(1, 256, 512)
+        load(1, 512, 768)
+        for h in range(2):
+            es = slice(h * E // 2, (h + 1) * E // 2)
+            ts = slice(h * E, (h + 1) * E)
+            nc.sync.dma_start(w_codes[:, ts, :].bitcast(I32), w_words[es].rearrange("e a p b -> p (e a) b").bitcast(I32))
+        for q in range(4):
+            nc.sync.dma_start(
+                w_plane[32 * q : 32 * q + 4, :, :].bitcast(I32),
+                w_scales[:, :, 4 * q : 4 * q + 4, :].rearrange("e a r n -> r (e a) n").bitcast(I32),
+            )
+        nc.sync.dma_start(bias[:], b)
+
+        cast("v", 0, 0, 0, 256)
+        cast("s", 0, 0, 256, 512)
+        quantise(0, 0, 256)
+        cast("v", 0, 512, 512, 672)
+        cast("s", 0, 512, 672, 768)
+        quantise(0, 256, 512)
+        quantise(0, 512, 768)
+
+        def gather_codes(a, s0, s1):
+            nc.vector.tensor_copy(slot_codes[a][:, s0:s1], codes[a][:].indirect(offsets[:, s0 // 16 : s1 // 16]))
+
+        def gather_scales(s0, s1):
+            nc.vector.tensor_copy(slot_plane[:, s0:s1], plane[:].indirect(offsets[:, s0 // 16 : s1 // 16]))
+            for q in range(4):
+                nc.sync.dma_start(
+                    slot_plane1[32 * q : 32 * q + 4, s0:s1].bitcast(I32),
+                    slot_plane[32 * q + 4 : 32 * q + 8, s0:s1].bitcast(I32),
+                )
+
+        gather_codes(0, 0, S)
+        cast("s", 1, 0, 0, 256)
+        cast("s", 1, 256, 256, 512)
+        quantise(1, 0, 512)
+        cast("s", 1, 512, 512, 768)
+        quantise(1, 512, 768)
+        for s0 in range(0, S, 512):
+            gather_scales(s0, s0 + 512)
+
+        acc = {}
+        scales = [slot_plane, slot_plane1]
+
+        def multiply(e, a):
+            if a == 0:
+                acc[e] = psum.tile([P, C], F32, name="acc")
+            cols = slice(e * C, (e + 1) * C)
+            nc.tensor.matmul_mx(
+                out=acc[e][:],
+                lhsT=w_codes[:, e * PASSES + a, :].bitcast(FP4X4),
+                lhsT_scale=w_plane[:, e * PASSES + a, :],
+                rhs=slot_codes[a][:, cols].bitcast(FP8X4),
+                rhs_scale=scales[a][:, cols],
+                start=(a == 0),
+                stop=(a == PASSES - 1),
+            )
+
+        out_view = out.rearrange("n (m e u) -> n m e u", m=R, e=E)
+
+        def finish(e0, e1, on_vector):
+            y = keep.tile([P, R, e1 - e0, U], F32, name=f"y{e0}")
+            for e in range(e0, e1):
+                dst = y[:, :, e - e0, :]
+                src = acc[e][:].rearrange("p (m u) -> p m u", m=R)
+                if e in on_vector:
+                    nc.vector.tensor_scalar_add(dst, src, bias[:, e : e + 1])
+                else:
+                    nc.scalar.activation(dst, src, IDENTITY, bias=bias[:, e : e + 1])
+            nc.sync.dma_start(out_view[:, :, e0:e1, :], y[:])
+
+        for e in range(8):
+            multiply(e, 0)
+        opened = 8
+        for e0, e1, ahead in ((0, 4, 4), (4, 8, 0), (8, 10, 0), (10, 12, 0)):
+            gather_codes(1, e0 * C, e1 * C)
+            for e in range(e0, e1):
+                multiply(e, 1)
+            finish(e0, e1, (11,))
+            for e in range(opened, opened + ahead):
+                multiply(e, 0)
+            opened += ahead

@@ -42,7 +42,7 @@ def tile_moe_eps_lin_bias_kernel(tc, xT, w_words, w_scales, b, offs, out):
 
         nc.gpsimd.memset(plane[:].bitcast(I32), 0)
         for a in range(PASSES):
-            nc.gpsimd.memset(codes[a][:, T:].bitcast(I32), 0)
+            nc.vector.memset(codes[a][:, T:].bitcast(I32), 0)
         nc.gpsimd.memset(slot_plane1[:].bitcast(I32), 0)
         nc.gpsimd.memset(w_plane[:].rearrange("p a n -> p (a n)").bitcast(I32), 0)
 
@@ -68,7 +68,8 @@ def tile_moe_eps_lin_bias_kernel(tc, xT, w_words, w_scales, b, offs, out):
                 in_=rounded[a][:, c0:c1, :].rearrange("p w j -> p (w j)"),
             )
 
-        load(0, 0, 512)
+        load(0, 0, 256)
+        load(0, 256, 512)
         load(0, 512, 768)
         nc.sync.dma_start(offsets[:], offs)
         load(1, 0, 256)
@@ -85,13 +86,14 @@ def tile_moe_eps_lin_bias_kernel(tc, xT, w_words, w_scales, b, offs, out):
             )
         nc.sync.dma_start(bias[:], b)
 
-        cast("v", 0, 0, 0, 256)
-        cast("s", 0, 0, 256, 512)
-        quantise(0, 0, 256)
-        cast("v", 0, 512, 512, 672)
-        cast("s", 0, 512, 672, 768)
-        quantise(0, 256, 512)
-        quantise(0, 512, 768)
+        for c0 in (0, 256):
+            cast("v", 0, c0, c0, c0 + 160)
+            cast("s", 0, c0, c0 + 160, c0 + 256)
+            quantise(0, c0, c0 + 256)
+        cast("v", 0, 512, 512, 640)
+        cast("s", 0, 512, 640, 768)
+        quantise(0, 512, 640)
+        quantise(0, 640, 768)
 
         def gather_codes(a, s0, s1):
             nc.vector.tensor_copy(slot_codes[a][:, s0:s1], codes[a][:].indirect(offsets[:, s0 // 16 : s1 // 16]))

@@ -31,7 +31,7 @@ def tile_moe_eps_lin_bias_kernel(tc, xT, w_words, w_scales, b, offs, out):
 
         offsets = keep.tile([P, S // 16], U16, name="offsets")
         plane = keep.tile([P, W], U8, name="plane", align_bytes=64)
-        w_codes = keep.tile([P, E * PASSES, 2 * N], U8, name="w_codes", align_bytes=64)
+        w_codes = [keep.tile([P, E, 2 * N], U8, name=f"w_codes{h}", align_bytes=64) for h in range(2)]
         w_plane = keep.tile([P, E * PASSES, N], U8, name="w_plane", align_bytes=64)
         bias = keep.tile([P, E], F32, name="bias")
         codes = [keep.tile([P, w], U32, name=f"codes{a}", align_bytes=64) for a, w in enumerate((2 * W, W))]
@@ -40,11 +40,11 @@ def tile_moe_eps_lin_bias_kernel(tc, xT, w_words, w_scales, b, offs, out):
         slot_plane1 = keep.tile([P, S], U8, name="slot_plane1", align_bytes=64)
         rounded = [keep.tile([P, T, 4], BF16, name=f"rounded{a}", align_bytes=64) for a in range(PASSES)]
 
+        nc.gpsimd.memset(w_plane[:].rearrange("p a n -> p (a n)").bitcast(I32), 0)
         nc.gpsimd.memset(plane[:].bitcast(I32), 0)
         for a in range(PASSES):
             nc.vector.memset(codes[a][:, T:].bitcast(I32), 0)
         nc.gpsimd.memset(slot_plane1[:].bitcast(I32), 0)
-        nc.gpsimd.memset(w_plane[:].rearrange("p a n -> p (a n)").bitcast(I32), 0)
 
         raw = {}
 
@@ -75,16 +75,15 @@ def tile_moe_eps_lin_bias_kernel(tc, xT, w_words, w_scales, b, offs, out):
         load(1, 0, 256)
         load(1, 256, 512)
         load(1, 512, 768)
+        nc.sync.dma_start(bias[:], b)
+        for r in range(4):
+            nc.sync.dma_start(
+                w_plane[r:P:32, :, :].bitcast(I32),
+                w_scales[:, :, r:16:4, :].rearrange("e a q n -> q (e a) n").bitcast(I32),
+            )
         for h in range(2):
             es = slice(h * E // 2, (h + 1) * E // 2)
-            ts = slice(h * E, (h + 1) * E)
-            nc.sync.dma_start(w_codes[:, ts, :].bitcast(I32), w_words[es].rearrange("e a p b -> p (e a) b").bitcast(I32))
-        for q in range(4):
-            nc.sync.dma_start(
-                w_plane[32 * q : 32 * q + 4, :, :].bitcast(I32),
-                w_scales[:, :, 4 * q : 4 * q + 4, :].rearrange("e a r n -> r (e a) n").bitcast(I32),
-            )
-        nc.sync.dma_start(bias[:], b)
+            nc.sync.dma_start(w_codes[h][:].bitcast(I32), w_words[es].rearrange("e a p b -> p (e a) b").bitcast(I32))
 
         for c0 in (0, 256):
             cast("v", 0, c0, c0, c0 + 160)
@@ -124,7 +123,7 @@ def tile_moe_eps_lin_bias_kernel(tc, xT, w_words, w_scales, b, offs, out):
             cols = slice(e * C, (e + 1) * C)
             nc.tensor.matmul_mx(
                 out=acc[e][:],
-                lhsT=w_codes[:, e * PASSES + a, :].bitcast(FP4X4),
+                lhsT=w_codes[e // 6][:, (e % 6) * PASSES + a, :].bitcast(FP4X4),
                 lhsT_scale=w_plane[:, e * PASSES + a, :],
                 rhs=slot_codes[a][:, cols].bitcast(FP8X4),
                 rhs_scale=scales[a][:, cols],

@@ -27,7 +27,7 @@ def tile_moe_eps_lin_bias_kernel(tc, xT, w_words, w_scales, b, offs, out):
     nc = tc.nc
     with ExitStack() as ctx:
         keep = ctx.enter_context(tc.tile_pool(name="keep", bufs=1))
-        psum = ctx.enter_context(tc.psum_pool(name="psum", bufs=8))
+        psum = ctx.enter_context(tc.psum_pool(name="psum", bufs=1))
 
         offsets = keep.tile([P, S // 16], U16, name="offsets")
         plane = keep.tile([P, W], U8, name="plane", align_bytes=64)
@@ -114,21 +114,26 @@ def tile_moe_eps_lin_bias_kernel(tc, xT, w_words, w_scales, b, offs, out):
         for s0 in range(0, S, 512):
             gather_scales(s0, s0 + 512)
 
-        acc = {}
+        banks = [(0, 1), (2, 3), (4, 5), (6, 7), (8,), (9,), (10,), (11,)]
+        acc, first, last = {}, set(), set()
+        for i, members in enumerate(banks):
+            bank = psum.tile([P, 512], F32, name=f"bank{i}")
+            first.add(members[0])
+            last.add(members[-1])
+            for j, e in enumerate(members):
+                acc[e] = bank[:, j * C : (j + 1) * C]
         scales = [slot_plane, slot_plane1]
 
         def multiply(e, a):
-            if a == 0:
-                acc[e] = psum.tile([P, C], F32, name="acc")
             cols = slice(e * C, (e + 1) * C)
             nc.tensor.matmul_mx(
-                out=acc[e][:],
+                out=acc[e],
                 lhsT=w_codes[e // 6][:, (e % 6) * PASSES + a, :].bitcast(FP4X4),
                 lhsT_scale=w_plane[:, e * PASSES + a, :],
                 rhs=slot_codes[a][:, cols].bitcast(FP8X4),
                 rhs_scale=scales[a][:, cols],
-                start=(a == 0),
-                stop=(a == PASSES - 1),
+                start=(a == 0 and e in first),
+                stop=(a == PASSES - 1 and e in last),
             )
 
         out_view = out.rearrange("n (m e u) -> n m e u", m=R, e=E)
@@ -137,21 +142,17 @@ def tile_moe_eps_lin_bias_kernel(tc, xT, w_words, w_scales, b, offs, out):
             y = keep.tile([P, R, e1 - e0, U], F32, name=f"y{e0}")
             for e in range(e0, e1):
                 dst = y[:, :, e - e0, :]
-                src = acc[e][:].rearrange("p (m u) -> p m u", m=R)
+                src = acc[e].rearrange("p (m u) -> p m u", m=R)
                 if e in on_vector:
                     nc.vector.tensor_scalar_add(dst, src, bias[:, e : e + 1])
                 else:
                     nc.scalar.activation(dst, src, IDENTITY, bias=bias[:, e : e + 1])
             nc.sync.dma_start(out_view[:, :, e0:e1, :], y[:])
 
-        for e in range(8):
+        for e in range(E):
             multiply(e, 0)
-        opened = 8
-        for e0, e1, ahead in ((0, 4, 4), (4, 8, 0), (8, 10, 0), (10, 12, 0)):
+        for e0, e1 in ((0, 4), (4, 8), (8, 10), (10, 12)):
             gather_codes(1, e0 * C, e1 * C)
             for e in range(e0, e1):
                 multiply(e, 1)
             finish(e0, e1, (11,))
-            for e in range(opened, opened + ahead):
-                multiply(e, 0)
-            opened += ahead

@@ -70,7 +70,8 @@ def tile_moe_eps_lin_bias_kernel(tc, xT, w_words, w_scales, b, offs, out):
 
         load(0, 0, 256)
         load(0, 256, 512)
-        load(0, 512, 768)
+        load(0, 512, 640)
+        load(0, 640, 768)
         nc.sync.dma_start(offsets[:], offs)
         load(1, 0, 256)
         load(1, 256, 512)
@@ -89,10 +90,10 @@ def tile_moe_eps_lin_bias_kernel(tc, xT, w_words, w_scales, b, offs, out):
             cast("v", 0, c0, c0, c0 + 160)
             cast("s", 0, c0, c0 + 160, c0 + 256)
             quantise(0, c0, c0 + 256)
-        cast("v", 0, 512, 512, 640)
-        cast("s", 0, 512, 640, 768)
-        quantise(0, 512, 640)
-        quantise(0, 640, 768)
+        for c0 in (512, 640):
+            cast("v", 0, c0, c0, c0 + 80)
+            cast("s", 0, c0, c0 + 80, c0 + 128)
+            quantise(0, c0, c0 + 128)
 
         def gather_codes(a, s0, s1):
             nc.vector.tensor_copy(slot_codes[a][:, s0:s1], codes[a][:].indirect(offsets[:, s0 // 16 : s1 // 16]))
@@ -151,8 +152,11 @@ def tile_moe_eps_lin_bias_kernel(tc, xT, w_words, w_scales, b, offs, out):
 
         for e in range(E):
             multiply(e, 0)
-        for e0, e1 in ((0, 4), (4, 8), (8, 10), (10, 12)):
+        for e0, e1 in ((0, 4), (4, 8), (8, 11), (11, 12)):
             gather_codes(1, e0 * C, e1 * C)
             for e in range(e0, e1):
                 multiply(e, 1)
-            finish(e0, e1, (11,))
+            if e1 <= 8:
+                finish(e0, e1, ())
+        finish(8, 10, (9,))
+        finish(10, 12, (11,))

@@ -30,7 +30,7 @@ def tile_moe_eps_lin_bias_kernel(tc, xT, w_words, w_scales, b, offs, out):
         psum = ctx.enter_context(tc.psum_pool(name="psum", bufs=1))
 
         offsets = keep.tile([P, S // 16], U16, name="offsets")
-        plane = keep.tile([P, W], U8, name="plane", align_bytes=64)
+        plane = keep.tile([P, 2 * W], U8, name="plane", align_bytes=64)
         w_codes = [keep.tile([P, E, 2 * N], U8, name=f"w_codes{h}", align_bytes=64) for h in range(2)]
         w_plane = keep.tile([P, E * PASSES, N], U8, name="w_plane", align_bytes=64)
         bias = keep.tile([P, E], F32, name="bias")
@@ -69,13 +69,13 @@ def tile_moe_eps_lin_bias_kernel(tc, xT, w_words, w_scales, b, offs, out):
             )
 
         load(0, 0, 256)
-        load(0, 256, 512)
-        load(0, 512, 640)
+        load(0, 384, 640)
+        load(0, 256, 384)
         load(0, 640, 768)
         nc.sync.dma_start(offsets[:], offs)
-        load(1, 0, 256)
-        load(1, 256, 512)
-        load(1, 512, 768)
+        order1 = (0, 128, 256, 512, 384, 640)
+        for c0 in order1:
+            load(1, c0, c0 + 128)
         nc.sync.dma_start(bias[:], b)
         for r in range(4):
             nc.sync.dma_start(
@@ -86,34 +86,39 @@ def tile_moe_eps_lin_bias_kernel(tc, xT, w_words, w_scales, b, offs, out):
             es = slice(h * E // 2, (h + 1) * E // 2)
             nc.sync.dma_start(w_codes[h][:].bitcast(I32), w_words[es].rearrange("e a p b -> p (e a) b").bitcast(I32))
 
-        for c0 in (0, 256):
+        for c0 in (0, 384):
             cast("v", 0, c0, c0, c0 + 160)
             cast("s", 0, c0, c0 + 160, c0 + 256)
             quantise(0, c0, c0 + 256)
-        for c0 in (512, 640):
+        for c0 in (256, 640):
             cast("v", 0, c0, c0, c0 + 80)
             cast("s", 0, c0, c0 + 80, c0 + 128)
             quantise(0, c0, c0 + 128)
 
-        def gather_codes(a, s0, s1):
-            nc.vector.tensor_copy(slot_codes[a][:, s0:s1], codes[a][:].indirect(offsets[:, s0 // 16 : s1 // 16]))
+        def gather(dst, table, s0, s1):
+            window = table[:, 0:512] if s1 <= U else table[:]
+            nc.vector.tensor_copy(dst[:, s0:s1], window.indirect(offsets[:, s0 // 16 : s1 // 16]))
 
-        def gather_scales(s0, s1):
-            nc.vector.tensor_copy(slot_plane[:, s0:s1], plane[:].indirect(offsets[:, s0 // 16 : s1 // 16]))
+        def gather_codes(a, s0, s1):
+            gather(slot_codes[a], codes[a], s0, s1)
+
+        def move_scales(s0, s1):
             for q in range(4):
                 nc.sync.dma_start(
                     slot_plane1[32 * q : 32 * q + 4, s0:s1].bitcast(I32),
                     slot_plane[32 * q + 4 : 32 * q + 8, s0:s1].bitcast(I32),
                 )
 
-        gather_codes(0, 0, S)
-        cast("s", 1, 0, 0, 256)
-        cast("s", 1, 256, 256, 512)
+        gather_codes(0, 0, U)
+        gather_codes(0, U, S)
+        for c0 in order1:
+            cast("s", 1, c0, c0, c0 + 128)
         quantise(1, 0, 512)
-        cast("s", 1, 512, 512, 768)
         quantise(1, 512, 768)
-        for s0 in range(0, S, 512):
-            gather_scales(s0, s0 + 512)
+        gather(slot_plane, plane, 0, U)
+        for s0, s1 in ((0, 512), (512, S)):
+            gather(slot_plane, plane, max(s0, U), s1)
+            move_scales(s0, s1)
 
         banks = [(0, 1), (2, 3), (4, 5), (6, 7), (8,), (9,), (10,), (11,)]
         acc, first, last = {}, set(), set()
@@ -125,6 +130,9 @@ def tile_moe_eps_lin_bias_kernel(tc, xT, w_words, w_scales, b, offs, out):
                 acc[e] = bank[:, j * C : (j + 1) * C]
         scales = [slot_plane, slot_plane1]
 
+        def opening(e):
+            return 1 if e < 4 else 0
+
         def multiply(e, a):
             cols = slice(e * C, (e + 1) * C)
             nc.tensor.matmul_mx(
@@ -133,8 +141,8 @@ def tile_moe_eps_lin_bias_kernel(tc, xT, w_words, w_scales, b, offs, out):
                 lhsT_scale=w_plane[:, e * PASSES + a, :],
                 rhs=slot_codes[a][:, cols].bitcast(FP8X4),
                 rhs_scale=scales[a][:, cols],
-                start=(a == 0 and e in first),
-                stop=(a == PASSES - 1 and e in last),
+                start=(a == opening(e) and e in first),
+                stop=(a != opening(e) and e in last),
             )
 
         out_view = out.rearrange("n (m e u) -> n m e u", m=R, e=E)
@@ -150,13 +158,21 @@ def tile_moe_eps_lin_bias_kernel(tc, xT, w_words, w_scales, b, offs, out):
                     nc.scalar.activation(dst, src, IDENTITY, bias=bias[:, e : e + 1])
             nc.sync.dma_start(out_view[:, :, e0:e1, :], y[:])
 
-        for e in range(E):
+        for e in range(4, E):
             multiply(e, 0)
         for e0, e1 in ((0, 4), (4, 8), (8, 11), (11, 12)):
             gather_codes(1, e0 * C, e1 * C)
-            for e in range(e0, e1):
-                multiply(e, 1)
+            if e0 > 0:
+                for e in range(e0, e1):
+                    multiply(e, 1)
+            else:
+                for e in range(e0, e1, 2):
+                    multiply(e, 1)
+                    multiply(e + 1, 1)
+                    multiply(e, 0)
+                    multiply(e + 1, 0)
             if e1 <= 8:
-                finish(e0, e1, ())
+                finish(e0, e0 + 2, ())
+                finish(e0 + 2, e1, ())
         finish(8, 10, (9,))
         finish(10, 12, (11,))

@@ -40,11 +40,11 @@ def tile_moe_eps_lin_bias_kernel(tc, xT, w_words, w_scales, b, offs, out):
         slot_plane1 = keep.tile([P, S], U8, name="slot_plane1", align_bytes=64)
         rounded = [keep.tile([P, T, 4], BF16, name=f"rounded{a}", align_bytes=64) for a in range(PASSES)]
 
-        nc.gpsimd.memset(w_plane[:].rearrange("p a n -> p (a n)").bitcast(I32), 0)
-        nc.gpsimd.memset(plane[:].bitcast(I32), 0)
+        nc.vector.memset(w_plane[:].rearrange("p a n -> p (a n)").bitcast(I32), 0)
+        nc.vector.memset(plane[:].bitcast(I32), 0)
         for a in range(PASSES):
             nc.vector.memset(codes[a][:, T:].bitcast(I32), 0)
-        nc.gpsimd.memset(slot_plane1[:].bitcast(I32), 0)
+        nc.vector.memset(slot_plane1[:].bitcast(I32), 0)
 
         raw = {}
 
@@ -131,7 +131,7 @@ def tile_moe_eps_lin_bias_kernel(tc, xT, w_words, w_scales, b, offs, out):
         scales = [slot_plane, slot_plane1]
 
         def opening(e):
-            return 1 if e < 4 else 0
+            return 1 if e in (2, 3) else 0
 
         def multiply(e, a):
             cols = slice(e * C, (e + 1) * C)
@@ -158,21 +158,18 @@ def tile_moe_eps_lin_bias_kernel(tc, xT, w_words, w_scales, b, offs, out):
                     nc.scalar.activation(dst, src, IDENTITY, bias=bias[:, e : e + 1])
             nc.sync.dma_start(out_view[:, :, e0:e1, :], y[:])
 
-        for e in range(4, E):
-            multiply(e, 0)
+        for e in range(E):
+            if opening(e) == 0:
+                multiply(e, 0)
         for e0, e1 in ((0, 4), (4, 8), (8, 11), (11, 12)):
             gather_codes(1, e0 * C, e1 * C)
-            if e0 > 0:
-                for e in range(e0, e1):
-                    multiply(e, 1)
-            else:
-                for e in range(e0, e1, 2):
-                    multiply(e, 1)
-                    multiply(e + 1, 1)
+            for e in range(e0, e1):
+                multiply(e, 1)
+            for e in range(e0, e1):
+                if opening(e) == 1:
                     multiply(e, 0)
-                    multiply(e + 1, 0)
             if e1 <= 8:
                 finish(e0, e0 + 2, ())
                 finish(e0 + 2, e1, ())
-        finish(8, 10, (9,))
+        finish(8, 10, (8,))
         finish(10, 12, (11,))

@@ -41,9 +41,6 @@ def tile_moe_eps_lin_bias_kernel(tc, xT, w_words, w_scales, b, offs, out):
         rounded = [keep.tile([P, T, 4], BF16, name=f"rounded{a}", align_bytes=64) for a in range(PASSES)]
 
         nc.vector.memset(w_plane[:].rearrange("p a n -> p (a n)").bitcast(I32), 0)
-        nc.vector.memset(plane[:].bitcast(I32), 0)
-        for a in range(PASSES):
-            nc.vector.memset(codes[a][:, T:].bitcast(I32), 0)
         nc.vector.memset(slot_plane1[:].bitcast(I32), 0)
 
         raw = {}
@@ -120,18 +117,25 @@ def tile_moe_eps_lin_bias_kernel(tc, xT, w_words, w_scales, b, offs, out):
             gather(slot_plane, plane, max(s0, U), s1)
             move_scales(s0, s1)
 
-        banks = [(0, 1), (2, 3), (4, 5), (6, 7), (8,), (9,), (10,), (11,)]
+        banks = [(0, 1), (2, 3), (4, 5), (8, 9), (6,), (7,), (10,), (11,)]
+        pieces = ((0, 4), (4, 8), (8, 10), (10, 12))
+        held = (2, 3)
+        stores = [(e, e + 2) for e in range(0, E, 2)]
+        on_vector = (7, 8, 9, 11)
+
+        order = [(e, 0) for e in range(E) if e not in held]
+        for e0, e1 in pieces:
+            order.extend((e, 1) for e in range(e0, e1))
+            order.extend((e, 0) for e in range(e0, e1) if e in held)
         acc, first, last = {}, set(), set()
         for i, members in enumerate(banks):
             bank = psum.tile([P, 512], F32, name=f"bank{i}")
-            first.add(members[0])
-            last.add(members[-1])
+            mine = [step for step in order if step[0] in members]
+            first.add(mine[0])
+            last.add(mine[-1])
             for j, e in enumerate(members):
                 acc[e] = bank[:, j * C : (j + 1) * C]
         scales = [slot_plane, slot_plane1]
-
-        def opening(e):
-            return 1 if e in (2, 3) else 0
 
         def multiply(e, a):
             cols = slice(e * C, (e + 1) * C)
@@ -141,13 +145,17 @@ def tile_moe_eps_lin_bias_kernel(tc, xT, w_words, w_scales, b, offs, out):
                 lhsT_scale=w_plane[:, e * PASSES + a, :],
                 rhs=slot_codes[a][:, cols].bitcast(FP8X4),
                 rhs_scale=scales[a][:, cols],
-                start=(a == opening(e) and e in first),
-                stop=(a != opening(e) and e in last),
+                start=(e, a) in first,
+                stop=(e, a) in last,
             )
 
-        out_view = out.rearrange("n (m e u) -> n m e u", m=R, e=E)
+        for e0, e1 in pieces:
+            gather_codes(1, e0 * C, e1 * C)
+        for e, a in order:
+            multiply(e, a)
 
-        def finish(e0, e1, on_vector):
+        out_view = out.rearrange("n (m e u) -> n m e u", m=R, e=E)
+        for e0, e1 in stores:
             y = keep.tile([P, R, e1 - e0, U], F32, name=f"y{e0}")
             for e in range(e0, e1):
                 dst = y[:, :, e - e0, :]
@@ -157,19 +165,3 @@ def tile_moe_eps_lin_bias_kernel(tc, xT, w_words, w_scales, b, offs, out):
                 else:
                     nc.scalar.activation(dst, src, IDENTITY, bias=bias[:, e : e + 1])
             nc.sync.dma_start(out_view[:, :, e0:e1, :], y[:])
-
-        for e in range(E):
-            if opening(e) == 0:
-                multiply(e, 0)
-        for e0, e1 in ((0, 4), (4, 8), (8, 11), (11, 12)):
-            gather_codes(1, e0 * C, e1 * C)
-            for e in range(e0, e1):
-                multiply(e, 1)
-            for e in range(e0, e1):
-                if opening(e) == 1:
-                    multiply(e, 0)
-            if e1 <= 8:
-                finish(e0, e0 + 2, ())
-                finish(e0 + 2, e1, ())
-        finish(8, 10, (8,))
-        finish(10, 12, (11,))

@@ -84,12 +84,12 @@ def tile_moe_eps_lin_bias_kernel(tc, xT, w_words, w_scales, b, offs, out):
             nc.sync.dma_start(w_codes[h][:].bitcast(I32), w_words[es].rearrange("e a p b -> p (e a) b").bitcast(I32))
 
         for c0 in (0, 384):
-            cast("v", 0, c0, c0, c0 + 160)
-            cast("s", 0, c0, c0 + 160, c0 + 256)
+            cast("v", 0, c0, c0, c0 + 128)
+            cast("s", 0, c0, c0 + 128, c0 + 256)
             quantise(0, c0, c0 + 256)
-        for c0 in (256, 640):
-            cast("v", 0, c0, c0, c0 + 80)
-            cast("s", 0, c0, c0 + 80, c0 + 128)
+        for c0, share in ((256, 64), (640, 80)):
+            cast("v", 0, c0, c0, c0 + share)
+            cast("s", 0, c0, c0 + share, c0 + 128)
             quantise(0, c0, c0 + 128)
 
         def gather(dst, table, s0, s1):

@@ -87,7 +87,7 @@ def tile_moe_eps_lin_bias_kernel(tc, xT, w_words, w_scales, b, offs, out):
             cast("v", 0, c0, c0, c0 + 128)
             cast("s", 0, c0, c0 + 128, c0 + 256)
             quantise(0, c0, c0 + 256)
-        for c0, share in ((256, 64), (640, 80)):
+        for c0, share in ((256, 64), (640, 64)):
             cast("v", 0, c0, c0, c0 + share)
             cast("s", 0, c0, c0 + share, c0 + 128)
             quantise(0, c0, c0 + 128)
@@ -117,11 +117,11 @@ def tile_moe_eps_lin_bias_kernel(tc, xT, w_words, w_scales, b, offs, out):
             gather(slot_plane, plane, max(s0, U), s1)
             move_scales(s0, s1)
 
-        banks = [(0, 1), (2, 3), (4, 5), (8, 9), (6,), (7,), (10,), (11,)]
-        pieces = ((0, 4), (4, 8), (8, 10), (10, 12))
+        banks = [(0, 1), (2, 3), (4, 5), (6, 7), (8,), (9,), (10,), (11,)]
+        pieces = ((0, 4), (4, 8), (8, 11), (11, 12))
         held = (2, 3)
         stores = [(e, e + 2) for e in range(0, E, 2)]
-        on_vector = (7, 8, 9, 11)
+        on_vector = (8, 11)
 
         order = [(e, 0) for e in range(E) if e not in held]
         for e0, e1 in pieces:

@@ -21,6 +21,7 @@ COPY = mybir.ActivationFunctionType.Copy
 IDENTITY = mybir.ActivationFunctionType.Identity
 
 W = 1024
+ZONE = 32 * 1024
 
 
 def tile_moe_eps_lin_bias_kernel(tc, xT, w_words, w_scales, b, offs, out):
@@ -29,16 +30,23 @@ def tile_moe_eps_lin_bias_kernel(tc, xT, w_words, w_scales, b, offs, out):
         keep = ctx.enter_context(tc.tile_pool(name="keep", bufs=1))
         psum = ctx.enter_context(tc.psum_pool(name="psum", bufs=1))
 
-        offsets = keep.tile([P, S // 16], U16, name="offsets")
-        plane = keep.tile([P, 2 * W], U8, name="plane", align_bytes=64)
-        w_codes = [keep.tile([P, E, 2 * N], U8, name=f"w_codes{h}", align_bytes=64) for h in range(2)]
-        w_plane = keep.tile([P, E * PASSES, N], U8, name="w_plane", align_bytes=64)
-        bias = keep.tile([P, E], F32, name="bias")
-        codes = [keep.tile([P, w], U32, name=f"codes{a}", align_bytes=64) for a, w in enumerate((2 * W, W))]
-        slot_codes = [keep.tile([P, S], U32, name=f"slot_codes{a}", align_bytes=64) for a in range(PASSES)]
-        slot_plane = keep.tile([P, S], U8, name="slot_plane", align_bytes=64)
-        slot_plane1 = keep.tile([P, S], U8, name="slot_plane1", align_bytes=64)
-        rounded = [keep.tile([P, T, 4], BF16, name=f"rounded{a}", align_bytes=64) for a in range(PASSES)]
+        used = [0] * 7
+
+        def place(zone, shape, dtype, nbytes, name):
+            at = used[zone]
+            used[zone] = at + (nbytes + 255) // 256 * 256
+            return keep.tile(shape, dtype, name=name, align_bytes=256, offset=zone * ZONE + at)
+
+        offsets = place(1, [P, S // 16], U16, S // 8, "offsets")
+        plane = place(0, [P, 2 * W], U8, 2 * W, "plane")
+        w_codes = [place(5, [P, E, 2 * N], U8, E * 2 * N, f"w_codes{h}") for h in range(2)]
+        w_plane = place(5, [P, E * PASSES, N], U8, E * PASSES * N, "w_plane")
+        bias = place(5, [P, E], F32, 4 * E, "bias")
+        codes = [place(0, [P, w], U32, 4 * w, f"codes{a}") for a, w in enumerate((2 * W, W))]
+        slot_codes = [place(2, [P, S], U32, 4 * S, f"slot_codes{a}") for a in range(PASSES)]
+        slot_plane = place(2, [P, S], U8, S, "slot_plane")
+        slot_plane1 = place(5, [P, S], U8, S, "slot_plane1")
+        rounded = [place(3, [P, T, 4], BF16, 8 * T, f"rounded{a}") for a in range(PASSES)]
 
         nc.vector.memset(w_plane[:].rearrange("p a n -> p (a n)").bitcast(I32), 0)
         nc.vector.memset(slot_plane1[:].bitcast(I32), 0)
@@ -46,7 +54,7 @@ def tile_moe_eps_lin_bias_kernel(tc, xT, w_words, w_scales, b, offs, out):
         raw = {}
 
         def load(a, c0, c1):
-            t = keep.tile([P, 4, c1 - c0], F32, name=f"raw{a}_{c0}")
+            t = place(4, [P, 4, c1 - c0], F32, 16 * (c1 - c0), f"raw{a}_{c0}")
             nc.sync.dma_start(t[:], xT[512 * a : 512 * a + 512, c0:c1].rearrange("(p j) w -> p j w", j=4))
             raw[a, c0] = t
 
@@ -156,7 +164,7 @@ def tile_moe_eps_lin_bias_kernel(tc, xT, w_words, w_scales, b, offs, out):
 
         out_view = out.rearrange("n (m e u) -> n m e u", m=R, e=E)
         for e0, e1 in stores:
-            y = keep.tile([P, R, e1 - e0, U], F32, name=f"y{e0}")
+            y = place(6, [P, R, e1 - e0, U], F32, 4 * C * (e1 - e0), f"y{e0}")
             for e in range(e0, e1):
                 dst = y[:, :, e - e0, :]
                 src = acc[e].rearrange("p (m u) -> p m u", m=R)

@@ -42,7 +42,7 @@ def tile_moe_eps_lin_bias_kernel(tc, xT, w_words, w_scales, b, offs, out):
         w_codes = [place(5, [P, E, 2 * N], U8, E * 2 * N, f"w_codes{h}") for h in range(2)]
         w_plane = place(5, [P, E * PASSES, N], U8, E * PASSES * N, "w_plane")
         bias = place(5, [P, E], F32, 4 * E, "bias")
-        codes = [place(0, [P, w], U32, 4 * w, f"codes{a}") for a, w in enumerate((2 * W, W))]
+        codes = [place(0, [P, w], U32, 4 * w, f"codes{a}") for a, w in enumerate((W, W))]
         slot_codes = [place(2, [P, S], U32, 4 * S, f"slot_codes{a}") for a in range(PASSES)]
         slot_plane = place(2, [P, S], U8, S, "slot_plane")
         slot_plane1 = place(5, [P, S], U8, S, "slot_plane1")
@@ -74,13 +74,13 @@ def tile_moe_eps_lin_bias_kernel(tc, xT, w_words, w_scales, b, offs, out):
             )
 
         load(0, 0, 256)
-        load(0, 384, 640)
         load(0, 256, 384)
-        load(0, 640, 768)
         nc.sync.dma_start(offsets[:], offs)
-        order1 = (0, 128, 256, 512, 384, 640)
-        for c0 in order1:
-            load(1, c0, c0 + 128)
+        for c0 in (384, 512, 640):
+            load(0, c0, c0 + 128)
+        order1 = [(c0, c0 + 128) for c0 in (0, 128, 256, 512, 384, 640)]
+        for c0, c1 in order1:
+            load(1, c0, c1)
         nc.sync.dma_start(bias[:], b)
         for r in range(4):
             nc.sync.dma_start(
@@ -91,33 +91,43 @@ def tile_moe_eps_lin_bias_kernel(tc, xT, w_words, w_scales, b, offs, out):
             es = slice(h * E // 2, (h + 1) * E // 2)
             nc.sync.dma_start(w_codes[h][:].bitcast(I32), w_words[es].rearrange("e a p b -> p (e a) b").bitcast(I32))
 
-        for c0 in (0, 384):
-            cast("v", 0, c0, c0, c0 + 128)
-            cast("s", 0, c0, c0 + 128, c0 + 256)
-            quantise(0, c0, c0 + 256)
-        for c0, share in ((256, 64), (640, 64)):
-            cast("v", 0, c0, c0, c0 + share)
-            cast("s", 0, c0, c0 + share, c0 + 128)
-            quantise(0, c0, c0 + 128)
-
         def gather(dst, table, s0, s1):
-            window = table[:, 0:512] if s1 <= U else table[:]
+            window = table[:, 0:512] if s1 - s0 == U and s0 % C == 0 else table[:]
             nc.vector.tensor_copy(dst[:, s0:s1], window.indirect(offsets[:, s0 // 16 : s1 // 16]))
 
         def gather_codes(a, s0, s1):
             gather(slot_codes[a], codes[a], s0, s1)
 
         def move_scales(s0, s1):
-            for q in range(4):
+            runs = ((0, 64), (64, 4), (96, 4)) if s0 == 0 else [(32 * q, 4) for q in range(4)]
+            for p0, rows in runs:
                 nc.sync.dma_start(
-                    slot_plane1[32 * q : 32 * q + 4, s0:s1].bitcast(I32),
-                    slot_plane[32 * q + 4 : 32 * q + 8, s0:s1].bitcast(I32),
+                    slot_plane1[p0 : p0 + rows, s0:s1].bitcast(I32),
+                    slot_plane[p0 + 4 : p0 + 4 + rows, s0:s1].bitcast(I32),
                 )
 
+        def cast_shared(c0, share, c1):
+            cast("v", 0, c0, c0, c0 + share)
+            cast("s", 0, c0, c0 + share, c1)
+
+        early = (3, 5, 8, 10)
+        cast_shared(0, 160, 256)
+        cast_shared(256, 64, 384)
+        quantise(0, 0, 256)
+        quantise(0, 256, 384)
+        for e in early:
+            gather_codes(0, e * C, e * C + U)
+        cast("s", 0, 384, 384, 512)
+        cast("s", 0, 512, 512, 640)
+        cast_shared(640, 64, 768)
+        quantise(0, 384, 640)
+        quantise(0, 640, 768)
         gather_codes(0, 0, U)
-        gather_codes(0, U, S)
-        for c0 in order1:
-            cast("s", 1, c0, c0, c0 + 128)
+        cuts = (0,) + early + (E,)
+        for e0, e1 in zip(cuts, cuts[1:]):
+            gather_codes(0, e0 * C + U, e1 * C)
+        for c0, c1 in order1:
+            cast("s", 1, c0, c0, c1)
         quantise(1, 0, 512)
         quantise(1, 512, 768)
         gather(slot_plane, plane, 0, U)

@@ -131,13 +131,13 @@ def tile_moe_eps_lin_bias_kernel(tc, xT, w_words, w_scales, b, offs, out):
         quantise(1, 0, 512)
         quantise(1, 512, 768)
         gather(slot_plane, plane, 0, U)
-        for s0, s1 in ((0, 512), (512, S)):
+        for s0, s1 in ((0, 8 * C), (8 * C, S)):
             gather(slot_plane, plane, max(s0, U), s1)
             move_scales(s0, s1)
 
         banks = [(0, 1), (2, 3), (4, 5), (6, 7), (8,), (9,), (10,), (11,)]
         pieces = ((0, 4), (4, 8), (8, 11), (11, 12))
-        held = (2, 3)
+        held = ()
         stores = [(e, e + 2) for e in range(0, E, 2)]
         on_vector = (8, 11)
 

@@ -76,7 +76,7 @@ def tile_moe_eps_lin_bias_kernel(tc, xT, w_words, w_scales, b, offs, out):
         load(0, 0, 256)
         load(0, 256, 384)
         nc.sync.dma_start(offsets[:], offs)
-        for c0 in (384, 512, 640):
+        for c0 in (512, 384, 640):
             load(0, c0, c0 + 128)
         order1 = [(c0, c0 + 128) for c0 in (0, 128, 256, 512, 384, 640)]
         for c0, c1 in order1:
@@ -115,12 +115,13 @@ def tile_moe_eps_lin_bias_kernel(tc, xT, w_words, w_scales, b, offs, out):
         cast_shared(256, 64, 384)
         quantise(0, 0, 256)
         quantise(0, 256, 384)
+        cast("s", 0, 512, 512, 640)
+        cast("s", 0, 384, 384, 512)
+        cast_shared(640, 64, 768)
         for e in early:
             gather_codes(0, e * C, e * C + U)
-        cast("s", 0, 384, 384, 512)
-        cast("s", 0, 512, 512, 640)
-        cast_shared(640, 64, 768)
-        quantise(0, 384, 640)
+        quantise(0, 512, 640)
+        quantise(0, 384, 512)
         quantise(0, 640, 768)
         gather_codes(0, 0, U)
         cuts = (0,) + early + (E,)
@@ -128,8 +129,9 @@ def tile_moe_eps_lin_bias_kernel(tc, xT, w_words, w_scales, b, offs, out):
             gather_codes(0, e0 * C + U, e1 * C)
         for c0, c1 in order1:
             cast("s", 1, c0, c0, c1)
+        quantise(1, 512, 640)
         quantise(1, 0, 512)
-        quantise(1, 512, 768)
+        quantise(1, 640, 768)
         gather(slot_plane, plane, 0, U)
         for s0, s1 in ((0, 8 * C), (8 * C, S)):
             gather(slot_plane, plane, max(s0, U), s1)

@@ -49,7 +49,7 @@ def tile_moe_eps_lin_bias_kernel(tc, xT, w_words, w_scales, b, offs, out):
         rounded = [place(3, [P, T, 4], BF16, 8 * T, f"rounded{a}") for a in range(PASSES)]
 
         nc.vector.memset(w_plane[:].rearrange("p a n -> p (a n)").bitcast(I32), 0)
-        nc.vector.memset(slot_plane1[:].bitcast(I32), 0)
+        nc.vector.memset(slot_plane1[96:P, :].bitcast(I32), 0)
 
         raw = {}
 
@@ -99,8 +99,7 @@ def tile_moe_eps_lin_bias_kernel(tc, xT, w_words, w_scales, b, offs, out):
             gather(slot_codes[a], codes[a], s0, s1)
 
         def move_scales(s0, s1):
-            runs = ((0, 64), (64, 4), (96, 4)) if s0 == 0 else [(32 * q, 4) for q in range(4)]
-            for p0, rows in runs:
+            for p0, rows in ((0, 64), (64, 32), (96, 4)):
                 nc.sync.dma_start(
                     slot_plane1[p0 : p0 + rows, s0:s1].bitcast(I32),
                     slot_plane[p0 + 4 : p0 + 4 + rows, s0:s1].bitcast(I32),
@@ -140,7 +139,7 @@ def tile_moe_eps_lin_bias_kernel(tc, xT, w_words, w_scales, b, offs, out):
         banks = [(0, 1), (2, 3), (4, 5), (6, 7), (8,), (9,), (10,), (11,)]
         pieces = ((0, 4), (4, 8), (8, 11), (11, 12))
         held = ()
-        stores = [(e, e + 2) for e in range(0, E, 2)]
+        stores = [(0, 1), (1, 2)] + [(e, e + 2) for e in range(2, E, 2)]
         on_vector = (8, 11)
 
         order = [(e, 0) for e in range(E) if e not in held]

@@ -43,8 +43,8 @@ def tile_moe_eps_lin_bias_kernel(tc, xT, w_words, w_scales, b, offs, out):
         w_plane = place(5, [P, E * PASSES, N], U8, E * PASSES * N, "w_plane")
         bias = place(5, [P, E], F32, 4 * E, "bias")
         codes = [place(0, [P, w], U32, 4 * w, f"codes{a}") for a, w in enumerate((W, W))]
-        slot_codes = [place(2, [P, S], U32, 4 * S, f"slot_codes{a}") for a in range(PASSES)]
-        slot_plane = place(2, [P, S], U8, S, "slot_plane")
+        slot_codes = [place(4, [P, S], U32, 4 * S, f"slot_codes{a}") for a in range(PASSES)]
+        slot_plane = place(4, [P, S], U8, S, "slot_plane")
         slot_plane1 = place(5, [P, S], U8, S, "slot_plane1")
         rounded = [place(3, [P, T, 4], BF16, 8 * T, f"rounded{a}") for a in range(PASSES)]
 
@@ -54,7 +54,7 @@ def tile_moe_eps_lin_bias_kernel(tc, xT, w_words, w_scales, b, offs, out):
         raw = {}
 
         def load(a, c0, c1):
-            t = place(4, [P, 4, c1 - c0], F32, 16 * (c1 - c0), f"raw{a}_{c0}")
+            t = place(2, [P, 4, c1 - c0], F32, 16 * (c1 - c0), f"raw{a}_{c0}")
             nc.sync.dma_start(t[:], xT[512 * a : 512 * a + 512, c0:c1].rearrange("(p j) w -> p j w", j=4))
             raw[a, c0] = t
 
@@ -132,7 +132,7 @@ def tile_moe_eps_lin_bias_kernel(tc, xT, w_words, w_scales, b, offs, out):
         quantise(1, 0, 512)
         quantise(1, 640, 768)
         gather(slot_plane, plane, 0, U)
-        for s0, s1 in ((0, 8 * C), (8 * C, S)):
+        for s0, s1 in ((0, 7 * C), (7 * C, S)):
             gather(slot_plane, plane, max(s0, U), s1)
             move_scales(s0, s1)
 

@@ -32,9 +32,12 @@ def tile_moe_eps_lin_bias_kernel(tc, xT, w_words, w_scales, b, offs, out):
 
         used = [0] * 7
 
+        where = {}
+
         def place(zone, shape, dtype, nbytes, name):
             at = used[zone]
             used[zone] = at + (nbytes + 255) // 256 * 256
+            where[name] = zone * ZONE + at
             return keep.tile(shape, dtype, name=name, align_bytes=256, offset=zone * ZONE + at)
 
         offsets = place(1, [P, S // 16], U16, S // 8, "offsets")
@@ -122,8 +125,8 @@ def tile_moe_eps_lin_bias_kernel(tc, xT, w_words, w_scales, b, offs, out):
         quantise(0, 512, 640)
         quantise(0, 384, 512)
         quantise(0, 640, 768)
-        gather_codes(0, 0, U)
-        cuts = (0,) + early + (E,)
+        gather_codes(0, C, C + U)
+        cuts = (1,) + early + (E,)
         for e0, e1 in zip(cuts, cuts[1:]):
             gather_codes(0, e0 * C + U, e1 * C)
         for c0, c1 in order1:
@@ -131,9 +134,10 @@ def tile_moe_eps_lin_bias_kernel(tc, xT, w_words, w_scales, b, offs, out):
         quantise(1, 512, 640)
         quantise(1, 0, 512)
         quantise(1, 640, 768)
-        gather(slot_plane, plane, 0, U)
+        first_codes = keep.tile([P, C], U32, name="first_codes", align_bytes=256, offset=where["raw1_640"])
+        gather(first_codes, codes[0], 0, C)
         for s0, s1 in ((0, 7 * C), (7 * C, S)):
-            gather(slot_plane, plane, max(s0, U), s1)
+            gather(slot_plane, plane, s0, s1)
             move_scales(s0, s1)
 
         banks = [(0, 1), (2, 3), (4, 5), (6, 7), (8,), (9,), (10,), (11,)]
@@ -162,7 +166,7 @@ def tile_moe_eps_lin_bias_kernel(tc, xT, w_words, w_scales, b, offs, out):
                 out=acc[e],
                 lhsT=w_codes[e // 6][:, (e % 6) * PASSES + a, :].bitcast(FP4X4),
                 lhsT_scale=w_plane[:, e * PASSES + a, :],
-                rhs=slot_codes[a][:, cols].bitcast(FP8X4),
+                rhs=(first_codes if (e, a) == (0, 0) else slot_codes[a])[:, cols].bitcast(FP8X4),
                 rhs_scale=scales[a][:, cols],
                 start=(e, a) in first,
                 stop=(e, a) in last,

@@ -81,7 +81,7 @@ def tile_moe_eps_lin_bias_kernel(tc, xT, w_words, w_scales, b, offs, out):
         nc.sync.dma_start(offsets[:], offs)
         for c0 in (512, 384, 640):
             load(0, c0, c0 + 128)
-        order1 = [(c0, c0 + 128) for c0 in (0, 128, 256, 512, 384, 640)]
+        order1 = [(c0, c0 + 128) for c0 in range(0, T, 128)]
         for c0, c1 in order1:
             load(1, c0, c1)
         nc.sync.dma_start(bias[:], b)
@@ -112,14 +112,14 @@ def tile_moe_eps_lin_bias_kernel(tc, xT, w_words, w_scales, b, offs, out):
             cast("v", 0, c0, c0, c0 + share)
             cast("s", 0, c0, c0 + share, c1)
 
-        early = (3, 5, 8, 10)
+        early = (4, 7, 10)
         cast_shared(0, 160, 256)
-        cast_shared(256, 64, 384)
+        cast_shared(256, 80, 384)
         quantise(0, 0, 256)
         quantise(0, 256, 384)
         cast("s", 0, 512, 512, 640)
         cast("s", 0, 384, 384, 512)
-        cast_shared(640, 64, 768)
+        cast_shared(640, 80, 768)
         for e in early:
             gather_codes(0, e * C, e * C + U)
         quantise(0, 512, 640)
@@ -131,9 +131,8 @@ def tile_moe_eps_lin_bias_kernel(tc, xT, w_words, w_scales, b, offs, out):
             gather_codes(0, e0 * C + U, e1 * C)
         for c0, c1 in order1:
             cast("s", 1, c0, c0, c1)
-        quantise(1, 512, 640)
         quantise(1, 0, 512)
-        quantise(1, 640, 768)
+        quantise(1, 512, 768)
         first_codes = keep.tile([P, C], U32, name="first_codes", align_bytes=256, offset=where["raw1_640"])
         gather(first_codes, codes[0], 0, C)
         for s0, s1 in ((0, 7 * C), (7 * C, S)):

@@ -132,7 +132,8 @@ def tile_moe_eps_lin_bias_kernel(tc, xT, w_words, w_scales, b, offs, out):
         for c0, c1 in order1:
             cast("s", 1, c0, c0, c1)
         quantise(1, 0, 512)
-        quantise(1, 512, 768)
+        quantise(1, 512, 640)
+        quantise(1, 640, 768)
         first_codes = keep.tile([P, C], U32, name="first_codes", align_bytes=256, offset=where["raw1_640"])
         gather(first_codes, codes[0], 0, C)
         for s0, s1 in ((0, 7 * C), (7 * C, S)):

from contextlib import ExitStack

import concourse.mybir as mybir

K, T, E, C, N, R = 1024, 768, 12, 128, 128, 2
P = 128
PASSES = 2
S = E * C
U = C // R
FLOPS = 2 * S * K * N

F32 = mybir.dt.float32
BF16 = mybir.dt.bfloat16
I32 = mybir.dt.int32
U32 = mybir.dt.uint32
U16 = mybir.dt.uint16
U8 = mybir.dt.uint8
FP8X4 = mybir.dt.float8_e4m3fn_x4
FP4X4 = mybir.dt.float4_e2m1fn_x4
COPY = mybir.ActivationFunctionType.Copy
IDENTITY = mybir.ActivationFunctionType.Identity

W = 1024
ZONE = 32 * 1024


def tile_moe_eps_lin_bias_kernel(tc, xT, w_words, w_scales, b, offs, out):
    nc = tc.nc
    with ExitStack() as ctx:
        keep = ctx.enter_context(tc.tile_pool(name="keep", bufs=1))
        psum = ctx.enter_context(tc.psum_pool(name="psum", bufs=1))

        used = [0] * 7

        where = {}

        def place(zone, shape, dtype, nbytes, name):
            at = used[zone]
            used[zone] = at + (nbytes + 255) // 256 * 256
            where[name] = zone * ZONE + at
            return keep.tile(shape, dtype, name=name, align_bytes=256, offset=zone * ZONE + at)

        offsets = place(1, [P, S // 16], U16, S // 8, "offsets")
        plane = place(0, [P, 2 * W], U8, 2 * W, "plane")
        w_codes = [place(5, [P, E, 2 * N], U8, E * 2 * N, f"w_codes{h}") for h in range(2)]
        w_plane = place(5, [P, E * PASSES, N], U8, E * PASSES * N, "w_plane")
        bias = place(5, [P, E], F32, 4 * E, "bias")
        codes = [place(0, [P, w], U32, 4 * w, f"codes{a}") for a, w in enumerate((W, W))]
        slot_codes = [place(4, [P, S], U32, 4 * S, f"slot_codes{a}") for a in range(PASSES)]
        slot_plane = place(4, [P, S], U8, S, "slot_plane")
        slot_plane1 = place(5, [P, S], U8, S, "slot_plane1")
        rounded = [place(3, [P, T, 4], BF16, 8 * T, f"rounded{a}") for a in range(PASSES)]

        nc.vector.memset(w_plane[:].rearrange("p a n -> p (a n)").bitcast(I32), 0)
        nc.vector.memset(slot_plane1[96:P, :].bitcast(I32), 0)

        raw = {}

        def load(a, c0, c1):
            t = place(2, [P, 4, c1 - c0], F32, 16 * (c1 - c0), f"raw{a}_{c0}")
            nc.sync.dma_start(t[:], xT[512 * a : 512 * a + 512, c0:c1].rearrange("(p j) w -> p j w", j=4))
            raw[a, c0] = t

        def cast(engine, a, base, c0, c1):
            src = raw[a, base][:, :, c0 - base : c1 - base].rearrange("p j (c i) -> p c j i", i=4)
            dst = rounded[a][:, c0:c1, :].rearrange("p (c i) j -> p c j i", i=4)
            if engine == "v":
                nc.vector.tensor_copy(dst, src)
            else:
                nc.scalar.activation(dst, src, COPY)

        def quantise(a, c0, c1):
            nc.vector.quantize_mx(
                out=codes[a][:, c0:c1].bitcast(FP8X4),
                scales=plane[4 * a : P, c0:c1],
                in_=rounded[a][:, c0:c1, :].rearrange("p w j -> p (w j)"),
            )

        load(0, 0, 256)
        load(0, 256, 384)
        nc.sync.dma_start(offsets[:], offs)
        for c0 in (512, 384, 640):
            load(0, c0, c0 + 128)
        order1 = [(c0, c0 + 128) for c0 in range(0, T, 128)]
        for c0, c1 in order1:
            load(1, c0, c1)
        nc.sync.dma_start(bias[:], b)
        for r in range(4):
            nc.sync.dma_start(
                w_plane[r:P:32, :, :].bitcast(I32),
                w_scales[:, :, r:16:4, :].rearrange("e a q n -> q (e a) n").bitcast(I32),
            )
        for h in range(2):
            es = slice(h * E // 2, (h + 1) * E // 2)
            nc.sync.dma_start(w_codes[h][:].bitcast(I32), w_words[es].rearrange("e a p b -> p (e a) b").bitcast(I32))

        def gather(dst, table, s0, s1):
            window = table[:, 0:512] if s1 - s0 == U and s0 % C == 0 else table[:]
            nc.vector.tensor_copy(dst[:, s0:s1], window.indirect(offsets[:, s0 // 16 : s1 // 16]))

        def gather_codes(a, s0, s1):
            gather(slot_codes[a], codes[a], s0, s1)

        def move_scales(s0, s1):
            for p0, rows in ((0, 64), (64, 32), (96, 4)):
                nc.sync.dma_start(
                    slot_plane1[p0 : p0 + rows, s0:s1].bitcast(I32),
                    slot_plane[p0 + 4 : p0 + 4 + rows, s0:s1].bitcast(I32),
                )

        def cast_shared(c0, share, c1):
            cast("v", 0, c0, c0, c0 + share)
            cast("s", 0, c0, c0 + share, c1)

        early = (4, 7, 10)
        cast_shared(0, 160, 256)
        cast_shared(256, 80, 384)
        quantise(0, 0, 256)
        quantise(0, 256, 384)
        cast("s", 0, 512, 512, 640)
        cast("s", 0, 384, 384, 512)
        cast_shared(640, 80, 768)
        for e in early:
            gather_codes(0, e * C, e * C + U)
        quantise(0, 512, 640)
        quantise(0, 384, 512)
        quantise(0, 640, 768)
        gather_codes(0, C, C + U)
        cuts = (1,) + early + (E,)
        for e0, e1 in zip(cuts, cuts[1:]):
            gather_codes(0, e0 * C + U, e1 * C)
        for c0, c1 in order1:
            cast("s", 1, c0, c0, c1)
        quantise(1, 0, 512)
        quantise(1, 512, 640)
        quantise(1, 640, 768)
        first_codes = keep.tile([P, C], U32, name="first_codes", align_bytes=256, offset=where["raw1_640"])
        gather(first_codes, codes[0], 0, C)
        for s0, s1 in ((0, 7 * C), (7 * C, S)):
            gather(slot_plane, plane, s0, s1)
            move_scales(s0, s1)

        banks = [(0, 1), (2, 3), (4, 5), (6, 7), (8,), (9,), (10,), (11,)]
        pieces = ((0, 4), (4, 8), (8, 11), (11, 12))
        held = ()
        stores = [(0, 1), (1, 2)] + [(e, e + 2) for e in range(2, E, 2)]
        on_vector = (8, 11)

        order = [(e, 0) for e in range(E) if e not in held]
        for e0, e1 in pieces:
            order.extend((e, 1) for e in range(e0, e1))
            order.extend((e, 0) for e in range(e0, e1) if e in held)
        acc, first, last = {}, set(), set()
        for i, members in enumerate(banks):
            bank = psum.tile([P, 512], F32, name=f"bank{i}")
            mine = [step for step in order if step[0] in members]
            first.add(mine[0])
            last.add(mine[-1])
            for j, e in enumerate(members):
                acc[e] = bank[:, j * C : (j + 1) * C]
        scales = [slot_plane, slot_plane1]

        def multiply(e, a):
            cols = slice(e * C, (e + 1) * C)
            nc.tensor.matmul_mx(
                out=acc[e],
                lhsT=w_codes[e // 6][:, (e % 6) * PASSES + a, :].bitcast(FP4X4),
                lhsT_scale=w_plane[:, e * PASSES + a, :],
                rhs=(first_codes if (e, a) == (0, 0) else slot_codes[a])[:, cols].bitcast(FP8X4),
                rhs_scale=scales[a][:, cols],
                start=(e, a) in first,
                stop=(e, a) in last,
            )

        for e0, e1 in pieces:
            gather_codes(1, e0 * C, e1 * C)
        for e, a in order:
            multiply(e, a)

        out_view = out.rearrange("n (m e u) -> n m e u", m=R, e=E)
        for e0, e1 in stores:
            y = place(6, [P, R, e1 - e0, U], F32, 4 * C * (e1 - e0), f"y{e0}")
            for e in range(e0, e1):
                dst = y[:, :, e - e0, :]
                src = acc[e].rearrange("p (m u) -> p m u", m=R)
                if e in on_vector:
                    nc.vector.tensor_scalar_add(dst, src, bias[:, e : e + 1])
                else:
                    nc.scalar.activation(dst, src, IDENTITY, bias=bias[:, e : e + 1])
            nc.sync.dma_start(out_view[:, :, e0:e1, :], y[:])
